import numpy as np
import ml_dtypes


def mxq(x, axis, fmt="e4m3"):
    dtype, down = {"e4m3": (ml_dtypes.float8_e4m3fn, 7), "e5m2": (ml_dtypes.float8_e5m2, 14)}[fmt]
    v = np.moveaxis(np.asarray(x, np.float32).astype(ml_dtypes.bfloat16).astype(np.float64), axis, -1)
    blocks = v.reshape(v.shape[:-1] + (-1, 32))
    amax = np.abs(blocks).max(-1, keepdims=True)
    byte = np.maximum(np.where(amax > 0, np.frexp(amax)[1] - 1 + 127, 0) - down, 1)
    scale = np.exp2(byte - 127.0)
    codes = (blocks / scale).astype(np.float32).astype(dtype).astype(np.float64)
    return np.moveaxis((codes * scale).reshape(v.shape), -1, axis)


WIDE = False


def mx_kscale(k):
    if not WIDE:
        return np.ones(k)
    levels = np.array([10, -10, 5, -5, 0])
    if k % 512:
        return np.exp2(np.random.permutation(np.resize(levels, k // 32))).repeat(32)
    a = np.empty((k // 512, 16))
    for p in range(k // 512):
        a[p, :8] = np.random.permutation(np.resize(levels, 8))
        for g in range(8):
            far = levels[np.abs(levels - a[p, g]) >= 10]
            a[p, g + 8] = far[np.random.randint(len(far))]
    return np.exp2(a.ravel()).repeat(32)


def f64(x):
    return np.asarray(x).astype(np.float64)


def striped(idx):
    return np.tile(np.asarray(idx).reshape(-1, 16).T, (8, 1)).astype(np.uint16)


def unstriped(offs):
    return offs[:16].T.reshape(-1).astype(np.int64)


E2M1 = np.array([0.0, 0.5, 1.0, 1.5, 2.0, 3.0, 4.0, 6.0, -0.0, -0.5, -1.0, -1.5, -2.0, -3.0, -4.0, -6.0])


def pack_weight(w, fmt):
    k, n = w.shape
    w = f64(np.asarray(w, np.float32).astype(ml_dtypes.bfloat16)).reshape(k // 32, 32, n)
    amax = np.abs(w).max(1)
    if fmt == "e4m3":
        byte = np.frexp(amax)[1] - 1 + 127 - 7
    else:
        mant, ex = np.frexp(amax / 6.0)
        byte = np.where(mant > 0.5, ex, ex - 1) + 127
    byte = np.clip(np.where(amax > 0, byte, 1), 1, 254)
    scaled = (w * np.exp2(127.0 - byte)[:, None, :]).reshape(k, n).astype(np.float32)
    by_word = np.ascontiguousarray(scaled.reshape(k // 512, 128, 4, n).transpose(0, 1, 3, 2))
    if fmt == "e4m3":
        words = by_word.astype(ml_dtypes.float8_e4m3fn).view(np.uint8)
    else:
        c = by_word.astype(ml_dtypes.float4_e2m1fn).view(np.uint8) & 0xF
        words = (c[..., 0::2] | (c[..., 1::2] << 4)).reshape(k // 512, 128, 2 * n)
    return np.ascontiguousarray(words), np.ascontiguousarray(byte.astype(np.uint8).reshape(k // 512, 16, n))


def unpack_weight(words, scales, fmt):
    g, _, n = scales.shape
    words = np.ascontiguousarray(words).reshape(g, 128, n, -1)
    if fmt == "e4m3":
        vals = words.view(ml_dtypes.float8_e4m3fn).astype(np.float64)
    else:
        nib = np.empty((g, 128, n, 4), np.uint8)
        nib[..., 0::2] = words & 0xF
        nib[..., 1::2] = words >> 4
        vals = E2M1[nib]
    vals = vals * np.repeat(np.exp2(scales.astype(np.float64) - 127.0), 8, axis=1)[..., None]
    return vals.transpose(0, 1, 3, 2).reshape(g * 512, n)


def bf(x):
    return np.asarray(x, np.float32).astype(ml_dtypes.bfloat16)


def planes(Y):
    r, m = Y.shape
    b = f64(bf(Y)).reshape(r // 32, 32, m)
    amax = np.abs(b).max(1)
    byte = np.clip(np.where(amax > 0, np.frexp(amax)[1] - 1 + 127 - 7, 1), 1, 254)
    codes = (b * np.exp2(127.0 - byte)[:, None, :]).reshape(r, m).astype(np.float32).astype(ml_dtypes.float8_e4m3fn).view(np.uint8)
    words = codes.reshape(r // 512, 128, 4, m).transpose(0, 1, 3, 2)
    return np.ascontiguousarray(words), np.ascontiguousarray(byte.astype(np.uint8).reshape(r // 512, 16, m))


D, T, I, Q, E = 512, 2048, 512, 256, 512


def setup_inputs():
    n = np.random.standard_normal
    idx = np.random.permutation(T)[:I]
    fd = mx_kscale(D)
    fi = mx_kscale(I)
    ti = np.ones(T)
    ti[idx] = fi
    keysp = pack_weight(n((D, T)) / fd[:, None], "e2m1")
    return {
        "query": (n((D, Q)) * 0.25 / np.sqrt(D) * fd[:, None]).astype(np.float32),
        "lquery": (n((D, Q)) * 0.8 / np.sqrt(D) * fd[:, None]).astype(np.float32),
        "keys_words": keysp[0],
        "keys_scales": keysp[1],
        "age": np.tile(np.random.uniform(0.0, 2.0, T), (128, 1)).astype(np.float32),
        "grace": (np.random.uniform(1.0, 2.0, (Q, 1))).astype(np.float32),
        "size": (np.random.uniform(0.5, 2.0, (1, I)) * fi).astype(np.float32),
        "vals": (n((E, T)) / ti).astype(np.float32),
        "offs": striped(idx),
    }


def reference(query, lquery, keys_words, keys_scales, age, grace, size, vals, offs):
    idx = unstriped(offs)
    keysu = unpack_weight(keys_words, keys_scales, "e2m1")
    queryq = mxq(f64(query), 0, "e4m3")
    keysidxg = keysu[:, idx]
    a = queryq.T @ keysidxg
    lqueryq = mxq(f64(lquery), 0, "e4m3")
    b = lqueryq.T @ keysidxg
    left = np.minimum(np.maximum(b + f64(grace) - f64(age)[:1][:, idx], 0.0), 1.0)
    p = np.exp(a - np.max(a, axis=1, keepdims=True)) * left
    w = p * f64(size) / np.sum(p, axis=1, keepdims=True)
    wt = w.T
    vt = f64(vals)[:, idx].T
    vtq = mxq(vt, 0, "e4m3")
    wtq = mxq(wt, 0, "e4m3")
    o = vtq.T @ wtq
    words, scales = planes(o)
    return o, words, scales

@@ -1,0 +1,231 @@
+from contextlib import ExitStack
+
+import concourse.mybir as mybir
+from concourse.masks import make_identity
+
+D, T, I, Q, E = 512, 2048, 512, 256, 512
+FLOPS = 2 * D * Q * I * 2 + 2 * I * E * Q
+BYTES = 4 * (2 * D * Q + T + Q + I + E * T + E * Q) + 128 * 2 * T + 16 * T + 128 * 64 + 128 * Q * 4 + 16 * Q
+
+F32 = mybir.dt.float32
+BF16 = mybir.dt.bfloat16
+I32 = mybir.dt.int32
+U32 = mybir.dt.uint32
+U16 = mybir.dt.uint16
+U8 = mybir.dt.uint8
+FP8X4 = mybir.dt.float8_e4m3fn_x4
+FP4X4 = mybir.dt.float4_e2m1fn_x4
+ACT = mybir.ActivationFunctionType
+ALU = mybir.AluOpType
+AXIS = mybir.AxisListType
+
+P = 128
+PACK = 4
+QT = Q // P
+
+
+def tile_attend_expiringslots_pl_kernel(
+    tc, query, lquery, keys_words, keys_scales, age, grace, size, vals, offs, out_0, out_1, out_2
+):
+    nc = tc.nc
+    with ExitStack() as ctx:
+        sb = ctx.enter_context(tc.tile_pool(name="sb", bufs=1))
+        ps = ctx.enter_context(tc.psum_pool(name="ps", bufs=1))
+
+        def tile(name, shape, dtype, tag=None):
+            return sb.tile(shape, dtype, name=name, tag=tag or name, align_bytes=64)
+
+        def bank(tag, name, shape):
+            return ps.tile(shape, F32, name=name, tag=tag)
+
+        offsets = tile("offsets", [P, I // 16], U16)
+        key_scale_pool = tile("key_scale_pool", [P, T], U8, tag="pool1")
+        age_pool = tile("age_pool", [P, T], F32, tag="pool3")
+        key_word_pool = tile("key_word_pool", [P, T], U16, tag="pool2")
+        lq_raw = tile("lq_raw", [P, PACK, Q], F32)
+        q_raw = tile("q_raw", [P, PACK, Q], F32)
+        grace_cols = tile("grace_cols", [P, QT], F32)
+        size_cols = tile("size_cols", [P, PACK], F32)
+        ident = tile("ident", [P, P], F32)
+
+        nc.vector.memset(key_scale_pool[:].bitcast(I32), 0)
+        nc.vector.memset(age_pool[:], 0.0)
+        nc.sync.dma_start(offsets[:], offs)
+        nc.sync.dma_start(key_word_pool[:].bitcast(I32), keys_words[0].bitcast(I32))
+        for g in range(4):
+            nc.scalar.dma_start(
+                key_scale_pool[32 * g : 32 * g + 4, :].bitcast(I32),
+                keys_scales[0, 4 * g : 4 * g + 4, :].bitcast(I32),
+            )
+        nc.scalar.dma_start(age_pool[0:1, :], age[0:1, :])
+        nc.sync.dma_start(lq_raw[:], lquery.rearrange("(p j) q -> p j q", j=PACK))
+        nc.sync.dma_start(q_raw[:], query.rearrange("(p j) q -> p j q", j=PACK))
+        vals_dealt = vals.rearrange("(p t) n -> t p n", t=PACK)
+
+        def load_values(t):
+            pool = tile("val_pool%d" % t, [P, T], F32, tag="pool%d" % t)
+            nc.sync.dma_start(pool[:], vals_dealt[t])
+            return pool
+
+        val_pools = [load_values(0)]
+        make_identity(nc, ident[:])
+        nc.gpsimd.dma_start(size_cols[:], size.rearrange("o (p c) -> p (o c)", c=PACK))
+        with nc.allow_non_contiguous_dma(reason="one grace to a partition"):
+            nc.gpsimd.dma_start(grace_cols[:], grace.rearrange("(c p) o -> p (c o)", p=P))
+
+        warm = tile("warm", [P, 1], F32)
+        nc.scalar.activation(warm[:], ident[:, 0:1], ACT.Exp)
+
+        key_scales = tile("key_scales", [P, I], U8)
+        key_words = tile("key_words", [P, I], U16)
+        nc.vector.tensor_copy(key_words[:], key_word_pool[:].indirect(offsets[:]))
+        nc.vector.tensor_copy(key_scales[:], key_scale_pool[:].indirect(offsets[:]))
+
+        val_pools.append(load_values(1))
+        val_pools.append(load_values(2))
+
+        def quantise_queries(name, raw):
+            grouped = tile(name + "_grouped", [P, Q, PACK], BF16)
+            codes = tile(name + "_codes", [P, Q], U32)
+            scales = tile(name + "_scales", [P, Q], U8)
+            nc.scalar.copy(
+                grouped[:].rearrange("p (c i) j -> p c j i", i=4),
+                raw[:].rearrange("p j (c i) -> p c j i", i=4),
+            )
+            nc.vector.quantize_mx(codes[:].bitcast(FP8X4), scales[:], grouped[:].rearrange("p q j -> p (q j)"))
+            return codes, scales
+
+        lq_codes, lq_scales = quantise_queries("lq", lq_raw)
+
+        age_row = tile("age_row", [P, I], F32)
+        nc.vector.tensor_copy(age_row[:], age_pool[:].indirect(offsets[:]))
+        val_pools.append(load_values(3))
+        age_ps = bank("turn", "age_ps", [P, 4, P])
+        for j in range(4):
+            nc.tensor.transpose(age_ps[:, j, :], age_row[:, P * j : P * (j + 1)], ident[:])
+        age_cols = tile("age_cols", [P, 4], F32)
+        nc.scalar.copy(age_cols[:], age_ps[:, :, 0])
+
+        q_codes, q_scales = quantise_queries("q", q_raw)
+
+        size_ps = bank("size", "size_ps", [P, PACK, P])
+        for c in range(PACK):
+            nc.tensor.transpose(size_ps[:, c, :], size_cols[:, c : c + 1].to_broadcast([P, P]), ident[:])
+
+        short = tile("short", [P, 4, Q], F32)
+        for h in range(2):
+            life_ps = bank("life%d" % h, "life_ps%d" % h, [P, 2, Q])
+            for jj in range(2):
+                cols = slice(P * (2 * h + jj), P * (2 * h + jj + 1))
+                nc.tensor.matmul_mx(
+                    life_ps[:, jj, :],
+                    lhsT=key_words[:, cols].bitcast(FP4X4),
+                    lhsT_scale=key_scales[:, cols],
+                    rhs=lq_codes[:].bitcast(FP8X4),
+                    rhs_scale=lq_scales[:],
+                    start=True,
+                    stop=True,
+                )
+            for jj in range(2):
+                j = 2 * h + jj
+                nc.scalar.activation(
+                    short[:, j, :], life_ps[:, jj, :], ACT.Identity, bias=age_cols[:, j : j + 1], scale=-1.0
+                )
+
+        exps = []
+        for c in range(QT):
+            cols = slice(P * c, P * (c + 1))
+            score_ps = bank("score%d" % c, "score_ps%d" % c, [P, I])
+            nc.tensor.matmul_mx(
+                score_ps[:],
+                lhsT=q_codes[:, cols].bitcast(FP8X4),
+                lhsT_scale=q_scales[:, cols],
+                rhs=key_words[:].bitcast(FP4X4),
+                rhs_scale=key_scales[:],
+                start=True,
+                stop=True,
+            )
+            neg_max = tile("neg_max%d" % c, [P, 1], F32)
+            nc.vector.tensor_reduce(neg_max[:], score_ps[:], AXIS.X, ALU.max, negate=True)
+            ex = tile("exp%d" % c, [P, I], F32)
+            nc.scalar.activation(ex[:], score_ps[:], ACT.Exp, bias=neg_max[:], scale=1.0)
+            exps.append(ex)
+
+        w_codes = tile("w_codes", [P, Q], U32)
+        w_scales = tile("w_scales", [P, Q], U8)
+        for c in range(QT):
+            cols = slice(P * c, P * (c + 1))
+            back_ps = bank("back%d" % c, "back_ps%d" % c, [P, I])
+            for j in range(4):
+                nc.tensor.transpose(back_ps[:, P * j : P * (j + 1)], short[:, j, cols], ident[:])
+            left = tile("left%d" % c, [P, I], F32)
+            nc.scalar.activation(left[:], back_ps[:], ACT.Relu, bias=grace_cols[:, c : c + 1], scale=-1.0)
+            p = tile("p%d" % c, [P, I], F32)
+            total = tile("total%d" % c, [P, 1], F32)
+            nc.vector.scalar_tensor_tensor(p[:], left[:], 1.0, exps[c][:], ALU.min, ALU.mult, accum_out=total[:])
+            inv = tile("inv%d" % c, [P, 1], F32)
+            nc.vector.reciprocal(inv[:], total[:])
+            w = tile("w%d" % c, [P, I], BF16)
+            nc.vector.scalar_tensor_tensor(
+                w[:].rearrange("q (s r) -> q s r", r=PACK),
+                p[:].rearrange("q (s r) -> q s r", r=PACK),
+                inv[:],
+                size_ps[:].rearrange("q r s -> q s r"),
+                ALU.mult,
+                ALU.mult,
+            )
+            wt_ps = bank("life%d" % c, "wt_ps%d" % c, [P, 2, P])
+            for u in range(2):
+                nc.tensor.transpose(wt_ps[:, u, :], w[:].bitcast(F32)[:, u::2], ident[:])
+            wt = tile("wt%d" % c, [P, P * PACK], BF16)
+            nc.scalar.copy(
+                wt[:].bitcast(F32).rearrange("s (q u) -> s q u", u=2), wt_ps[:].rearrange("s u q -> s q u")
+            )
+            nc.vector.quantize_mx(w_codes[:, cols].bitcast(FP8X4), w_scales[:, cols], wt[:])
+
+        out_ps = [bank("score%d" % c, "out_ps%d" % c, [P, PACK, P]) for c in range(QT)]
+        out_dealt = out_0.rearrange("(p t) q -> t p q", t=PACK)
+        for t in range(PACK):
+            picked = tile("picked%d" % t, [P, I], BF16)
+            nc.vector.tensor_copy(picked[:], val_pools[t][:].indirect(offsets[:]))
+            vt_ps = bank("turn", "vt_ps%d" % t, [P, 2, P])
+            for u in range(2):
+                nc.tensor.transpose(vt_ps[:, u, :], picked[:].bitcast(F32)[:, u::2], ident[:])
+            vt = tile("vt%d" % t, [P, P * PACK], BF16)
+            nc.scalar.copy(
+                vt[:].bitcast(F32).rearrange("s (e u) -> s e u", u=2), vt_ps[:].rearrange("s u e -> s e u")
+            )
+            v_codes = tile("v_codes%d" % t, [P, P], U32)
+            v_scales = tile("v_scales%d" % t, [P, P], U8)
+            nc.vector.quantize_mx(v_codes[:].bitcast(FP8X4), v_scales[:], vt[:])
+            for c in range(QT):
+                cols = slice(P * c, P * (c + 1))
+                nc.tensor.matmul_mx(
+                    out_ps[c][:, t, :],
+                    lhsT=v_codes[:].bitcast(FP8X4),
+                    lhsT_scale=v_scales[:],
+                    rhs=w_codes[:, cols].bitcast(FP8X4),
+                    rhs_scale=w_scales[:, cols],
+                    start=True,
+                    stop=True,
+                )
+            if t == PACK - 1:
+                o_grouped = tile("o_grouped", [P, QT, P, PACK], BF16)
+                nc.vector.tensor_copy(o_grouped[:, 0], out_ps[0][:].rearrange("p t q -> p q t"))
+                nc.scalar.copy(o_grouped[:, 1], out_ps[1][:].rearrange("p t q -> p q t"))
+            result = tile("result%d" % t, [P, Q], F32)
+            for c in range(QT):
+                nc.scalar.copy(result[:, P * c : P * (c + 1)], out_ps[c][:, t, :])
+            nc.sync.dma_start(out_dealt[t], result[:])
+
+        o_codes = tile("o_codes", [P, Q], U32)
+        o_scales = tile("o_scales", [P, Q], U8)
+        nc.vector.quantize_mx(
+            o_codes[:].bitcast(FP8X4), o_scales[:], o_grouped[:].rearrange("p c q t -> p (c q t)")
+        )
+        nc.sync.dma_start(out_1[0].rearrange("p c r -> p (c r)").bitcast(I32), o_codes[:].bitcast(I32))
+        for g in range(4):
+            queue = nc.sync if g % 2 == 0 else nc.scalar
+            queue.dma_start(
+                out_2[0, 4 * g : 4 * g + 4, :].bitcast(I32), o_scales[32 * g : 32 * g + 4, :].bitcast(I32)
+            )

@@ -39,27 +39,27 @@ def tile_attend_expiringslots_pl_kernel(
             return ps.tile(shape, F32, name=name, tag=tag)
 
         offsets = tile("offsets", [P, I // 16], U16)
-        key_scale_pool = tile("key_scale_pool", [P, T], U8, tag="pool1")
+        key_scale_pool = tile("key_scale_pool", [P, T], U8, tag="small")
+        lq_raw = tile("lq_raw", [P, PACK, Q], F32, tag="pool1")
         age_pool = tile("age_pool", [P, T], F32, tag="pool3")
-        key_word_pool = tile("key_word_pool", [P, T], U16, tag="pool2")
-        lq_raw = tile("lq_raw", [P, PACK, Q], F32)
-        q_raw = tile("q_raw", [P, PACK, Q], F32)
-        grace_cols = tile("grace_cols", [P, QT], F32)
-        size_cols = tile("size_cols", [P, PACK], F32)
+        key_word_pool = tile("key_word_pool", [P, T], U16, tag="pool0")
+        q_raw = tile("q_raw", [P, PACK, Q], F32, tag="pool2")
+        age_row = tile("age_row", [P, I], F32)
         ident = tile("ident", [P, P], F32)
 
-        nc.vector.memset(key_scale_pool[:].bitcast(I32), 0)
-        nc.vector.memset(age_pool[:], 0.0)
         nc.sync.dma_start(offsets[:], offs)
         nc.sync.dma_start(key_word_pool[:].bitcast(I32), keys_words[0].bitcast(I32))
+        nc.sync.dma_start(lq_raw[:], lquery.rearrange("(p j) q -> p j q", j=PACK))
+        nc.sync.dma_start(q_raw[:], query.rearrange("(p j) q -> p j q", j=PACK))
+        nc.gpsimd.memset(key_scale_pool[:].bitcast(I32), 0)
+        nc.vector.memset(age_pool[:].bitcast(I32), 0)
+        make_identity(nc, ident[:])
         for g in range(4):
             nc.scalar.dma_start(
                 key_scale_pool[32 * g : 32 * g + 4, :].bitcast(I32),
                 keys_scales[0, 4 * g : 4 * g + 4, :].bitcast(I32),
             )
         nc.scalar.dma_start(age_pool[0:1, :], age[0:1, :])
-        nc.sync.dma_start(lq_raw[:], lquery.rearrange("(p j) q -> p j q", j=PACK))
-        nc.sync.dma_start(q_raw[:], query.rearrange("(p j) q -> p j q", j=PACK))
         vals_dealt = vals.rearrange("(p t) n -> t p n", t=PACK)
 
         def load_values(t):
@@ -67,52 +67,61 @@ def tile_attend_expiringslots_pl_kernel(
             nc.sync.dma_start(pool[:], vals_dealt[t])
             return pool
 
-        val_pools = [load_values(0)]
-        make_identity(nc, ident[:])
-        nc.gpsimd.dma_start(size_cols[:], size.rearrange("o (p c) -> p (o c)", c=PACK))
-        with nc.allow_non_contiguous_dma(reason="one grace to a partition"):
-            nc.gpsimd.dma_start(grace_cols[:], grace.rearrange("(c p) o -> p (c o)", p=P))
-
-        warm = tile("warm", [P, 1], F32)
-        nc.scalar.activation(warm[:], ident[:, 0:1], ACT.Exp)
-
         key_scales = tile("key_scales", [P, I], U8)
         key_words = tile("key_words", [P, I], U16)
         nc.vector.tensor_copy(key_words[:], key_word_pool[:].indirect(offsets[:]))
         nc.vector.tensor_copy(key_scales[:], key_scale_pool[:].indirect(offsets[:]))
-
-        val_pools.append(load_values(1))
-        val_pools.append(load_values(2))
-
-        def quantise_queries(name, raw):
-            grouped = tile(name + "_grouped", [P, Q, PACK], BF16)
-            codes = tile(name + "_codes", [P, Q], U32)
-            scales = tile(name + "_scales", [P, Q], U8)
-            nc.scalar.copy(
-                grouped[:].rearrange("p (c i) j -> p c j i", i=4),
-                raw[:].rearrange("p j (c i) -> p c j i", i=4),
-            )
-            nc.vector.quantize_mx(codes[:].bitcast(FP8X4), scales[:], grouped[:].rearrange("p q j -> p (q j)"))
-            return codes, scales
-
-        lq_codes, lq_scales = quantise_queries("lq", lq_raw)
-
-        age_row = tile("age_row", [P, I], F32)
         nc.vector.tensor_copy(age_row[:], age_pool[:].indirect(offsets[:]))
-        val_pools.append(load_values(3))
+        val_pools = [load_values(0)]
+        small = tile("small", [P, 16], F32, tag="small")
+        size_cols = small[:, 0:PACK]
+        grace_cols = small[:, 8 : 8 + QT]
+        nc.sync.dma_start(size_cols, size.rearrange("o (p c) -> p (o c)", c=PACK))
+        with nc.allow_non_contiguous_dma(reason="one grace to a partition"):
+            nc.sync.dma_start(grace_cols, grace.rearrange("(c p) o -> p (c o)", p=P))
+
         age_ps = bank("turn", "age_ps", [P, 4, P])
         for j in range(4):
             nc.tensor.transpose(age_ps[:, j, :], age_row[:, P * j : P * (j + 1)], ident[:])
         age_cols = tile("age_cols", [P, 4], F32)
         nc.scalar.copy(age_cols[:], age_ps[:, :, 0])
 
-        q_codes, q_scales = quantise_queries("q", q_raw)
+        grouped = tile("q_grouped", [P, 2, Q, PACK], BF16)
+        for n, raw in enumerate((lq_raw, q_raw)):
+            nc.scalar.activation(
+                grouped[:, n].rearrange("p (c i) j -> p c j i", i=4),
+                raw[:].rearrange("p j (c i) -> p c j i", i=4),
+                ACT.Copy,
+            )
+        val_pools.append(load_values(1))
+        val_pools.append(load_values(2))
+        both_codes = tile("both_codes", [P, 2 * Q], U32, tag="pool3")
+        both_scales = tile("both_scales", [P, 2 * Q], U8)
+        nc.vector.quantize_mx(
+            both_codes[:].bitcast(FP8X4), both_scales[:], grouped[:].rearrange("p n q j -> p (n q j)")
+        )
+        lq_codes, lq_scales = both_codes[:, 0:Q], both_scales[:, 0:Q]
+        q_codes, q_scales = both_codes[:, Q : 2 * Q], both_scales[:, Q : 2 * Q]
 
-        size_ps = bank("size", "size_ps", [P, PACK, P])
-        for c in range(PACK):
-            nc.tensor.transpose(size_ps[:, c, :], size_cols[:, c : c + 1].to_broadcast([P, P]), ident[:])
+        def gather_values(t):
+            picked = tile("picked%d" % t, [P, I], BF16, tag=("q_grouped", "both_scales", None, "p1")[t])
+            nc.vector.tensor_copy(picked[:], val_pools[t][:].indirect(offsets[:]))
+            return picked
+
+        def turn_values(t, picked):
+            vt_ps = bank("turn", "vt_ps%d" % t, [P, 2, P])
+            for u in range(2):
+                nc.tensor.transpose(vt_ps[:, u, :], picked[:].bitcast(F32)[:, u::2], ident[:])
+            vt = tile("vt%d" % t, [P, P * PACK], BF16)
+            nc.scalar.copy(
+                vt[:].bitcast(F32).rearrange("s (e u) -> s e u", u=2), vt_ps[:].rearrange("s u e -> s e u")
+            )
+            return vt
+
+        picked0 = gather_values(0)
 
         short = tile("short", [P, 4, Q], F32)
+        score_banks = []
         for h in range(2):
             life_ps = bank("life%d" % h, "life_ps%d" % h, [P, 2, Q])
             for jj in range(2):
@@ -121,21 +130,13 @@ def tile_attend_expiringslots_pl_kernel(
                     life_ps[:, jj, :],
                     lhsT=key_words[:, cols].bitcast(FP4X4),
                     lhsT_scale=key_scales[:, cols],
-                    rhs=lq_codes[:].bitcast(FP8X4),
-                    rhs_scale=lq_scales[:],
+                    rhs=lq_codes.bitcast(FP8X4),
+                    rhs_scale=lq_scales,
                     start=True,
                     stop=True,
                 )
-            for jj in range(2):
-                j = 2 * h + jj
-                nc.scalar.activation(
-                    short[:, j, :], life_ps[:, jj, :], ACT.Identity, bias=age_cols[:, j : j + 1], scale=-1.0
-                )
-
-        exps = []
-        for c in range(QT):
-            cols = slice(P * c, P * (c + 1))
-            score_ps = bank("score%d" % c, "score_ps%d" % c, [P, I])
+            cols = slice(P * h, P * (h + 1))
+            score_ps = bank("score%d" % h, "score_ps%d" % h, [P, I])
             nc.tensor.matmul_mx(
                 score_ps[:],
                 lhsT=q_codes[:, cols].bitcast(FP8X4),
@@ -145,14 +146,29 @@ def tile_attend_expiringslots_pl_kernel(
                 start=True,
                 stop=True,
             )
-            neg_max = tile("neg_max%d" % c, [P, 1], F32)
-            nc.vector.tensor_reduce(neg_max[:], score_ps[:], AXIS.X, ALU.max, negate=True)
-            ex = tile("exp%d" % c, [P, I], F32)
-            nc.scalar.activation(ex[:], score_ps[:], ACT.Exp, bias=neg_max[:], scale=1.0)
-            exps.append(ex)
+            score_banks.append(score_ps)
+            for jj in range(2):
+                j = 2 * h + jj
+                nc.scalar.activation(
+                    short[:, j, :], life_ps[:, jj, :], ACT.Identity, bias=age_cols[:, j : j + 1], scale=-1.0
+                )
 
-        w_codes = tile("w_codes", [P, Q], U32)
-        w_scales = tile("w_scales", [P, Q], U8)
+        def exponentials(c):
+            neg_max = tile("neg_max%d" % c, [P, 1], F32, tag="pool0" if c == 0 else None)
+            nc.vector.tensor_reduce(neg_max[:], score_banks[c][:], AXIS.X, ALU.max, negate=True)
+            ex = tile("exp%d" % c, [P, I], F32)
+            nc.scalar.activation(ex[:], score_banks[c][:], ACT.Exp, bias=neg_max[:], scale=1.0)
+            return ex
+
+        exps = [exponentials(c) for c in range(QT)]
+
+        val_pools.append(load_values(3))
+        turned = [turn_values(0, picked0)]
+        picked1 = gather_values(1)
+        picked2 = gather_values(2)
+
+        ps_tiles = []
+        totals = tile("totals", [P, QT], F32)
         for c in range(QT):
             cols = slice(P * c, P * (c + 1))
             back_ps = bank("back%d" % c, "back_ps%d" % c, [P, I])
@@ -160,63 +176,79 @@ def tile_attend_expiringslots_pl_kernel(
                 nc.tensor.transpose(back_ps[:, P * j : P * (j + 1)], short[:, j, cols], ident[:])
             left = tile("left%d" % c, [P, I], F32)
             nc.scalar.activation(left[:], back_ps[:], ACT.Relu, bias=grace_cols[:, c : c + 1], scale=-1.0)
-            p = tile("p%d" % c, [P, I], F32)
-            total = tile("total%d" % c, [P, 1], F32)
-            nc.vector.scalar_tensor_tensor(p[:], left[:], 1.0, exps[c][:], ALU.min, ALU.mult, accum_out=total[:])
-            inv = tile("inv%d" % c, [P, 1], F32)
-            nc.vector.reciprocal(inv[:], total[:])
+            p = tile("p%d" % c, [P, I], F32, tag="pool2" if c == 0 else None)
+            nc.vector.scalar_tensor_tensor(
+                p[:], left[:], 1.0, exps[c][:], ALU.min, ALU.mult, accum_out=totals[:, c : c + 1]
+            )
+            ps_tiles.append(p)
+        turned.append(turn_values(1, picked1))
+        turned.append(turn_values(2, picked2))
+        size_ps = bank("life0", "size_ps", [P, PACK, P])
+        for c in range(PACK):
+            nc.tensor.transpose(size_ps[:, c, :], size_cols[:, c : c + 1].to_broadcast([P, P]), ident[:])
+
+        inv = tile("inv", [P, QT], F32)
+        nc.vector.reciprocal(inv[:], totals[:])
+        wt = tile("wt", [P, QT, P * PACK], BF16)
+        for c in range(QT):
             w = tile("w%d" % c, [P, I], BF16)
             nc.vector.scalar_tensor_tensor(
                 w[:].rearrange("q (s r) -> q s r", r=PACK),
-                p[:].rearrange("q (s r) -> q s r", r=PACK),
-                inv[:],
+                ps_tiles[c][:].rearrange("q (s r) -> q s r", r=PACK),
+                inv[:, c : c + 1],
                 size_ps[:].rearrange("q r s -> q s r"),
                 ALU.mult,
                 ALU.mult,
             )
-            wt_ps = bank("life%d" % c, "wt_ps%d" % c, [P, 2, P])
+            wt_ps = bank(("spare", "life1")[c], "wt_ps%d" % c, [P, 2, P])
             for u in range(2):
                 nc.tensor.transpose(wt_ps[:, u, :], w[:].bitcast(F32)[:, u::2], ident[:])
-            wt = tile("wt%d" % c, [P, P * PACK], BF16)
             nc.scalar.copy(
-                wt[:].bitcast(F32).rearrange("s (q u) -> s q u", u=2), wt_ps[:].rearrange("s u q -> s q u")
+                wt[:, c, :].bitcast(F32).rearrange("s (q u) -> s q u", u=2), wt_ps[:].rearrange("s u q -> s q u")
             )
-            nc.vector.quantize_mx(w_codes[:, cols].bitcast(FP8X4), w_scales[:, cols], wt[:])
+        picked3 = gather_values(3)
+        turned.append(turn_values(3, picked3))
+
+        def quantise_values(t):
+            v_codes = tile("v_codes%d" % t, [P, P], U32, tag=("left0", "left1", "pool2", None)[t])
+            v_scales = tile("v_scales%d" % t, [P, P], U8)
+            nc.vector.quantize_mx(v_codes[:].bitcast(FP8X4), v_scales[:], turned[t][:])
+            return v_codes, v_scales
+
+        v_mx = [quantise_values(t) for t in range(PACK - 1)]
+        w_codes = tile("w_codes", [P, Q], U32)
+        w_scales = tile("w_scales", [P, Q], U8)
+        for c in range(QT):
+            cols = slice(P * c, P * (c + 1))
+            nc.vector.quantize_mx(w_codes[:, cols].bitcast(FP8X4), w_scales[:, cols], wt[:, c, :])
+        v_mx.append(quantise_values(PACK - 1))
 
         out_ps = [bank("score%d" % c, "out_ps%d" % c, [P, PACK, P]) for c in range(QT)]
-        out_dealt = out_0.rearrange("(p t) q -> t p q", t=PACK)
-        for t in range(PACK):
-            picked = tile("picked%d" % t, [P, I], BF16)
-            nc.vector.tensor_copy(picked[:], val_pools[t][:].indirect(offsets[:]))
-            vt_ps = bank("turn", "vt_ps%d" % t, [P, 2, P])
-            for u in range(2):
-                nc.tensor.transpose(vt_ps[:, u, :], picked[:].bitcast(F32)[:, u::2], ident[:])
-            vt = tile("vt%d" % t, [P, P * PACK], BF16)
-            nc.scalar.copy(
-                vt[:].bitcast(F32).rearrange("s (e u) -> s e u", u=2), vt_ps[:].rearrange("s u e -> s e u")
+
+        def multiply(t, c):
+            cols = slice(P * c, P * (c + 1))
+            nc.tensor.matmul_mx(
+                out_ps[c][:, t, :],
+                lhsT=v_mx[t][0][:].bitcast(FP8X4),
+                lhsT_scale=v_mx[t][1][:],
+                rhs=w_codes[:, cols].bitcast(FP8X4),
+                rhs_scale=w_scales[:, cols],
+                start=True,
+                stop=True,
             )
-            v_codes = tile("v_codes%d" % t, [P, P], U32)
-            v_scales = tile("v_scales%d" % t, [P, P], U8)
-            nc.vector.quantize_mx(v_codes[:].bitcast(FP8X4), v_scales[:], vt[:])
-            for c in range(QT):
-                cols = slice(P * c, P * (c + 1))
-                nc.tensor.matmul_mx(
-                    out_ps[c][:, t, :],
-                    lhsT=v_codes[:].bitcast(FP8X4),
-                    lhsT_scale=v_scales[:],
-                    rhs=w_codes[:, cols].bitcast(FP8X4),
-                    rhs_scale=w_scales[:, cols],
-                    start=True,
-                    stop=True,
-                )
-            if t == PACK - 1:
-                o_grouped = tile("o_grouped", [P, QT, P, PACK], BF16)
-                nc.vector.tensor_copy(o_grouped[:, 0], out_ps[0][:].rearrange("p t q -> p q t"))
-                nc.scalar.copy(o_grouped[:, 1], out_ps[1][:].rearrange("p t q -> p q t"))
-            result = tile("result%d" % t, [P, Q], F32)
-            for c in range(QT):
-                nc.scalar.copy(result[:, P * c : P * (c + 1)], out_ps[c][:, t, :])
-            nc.sync.dma_start(out_dealt[t], result[:])
+
+        for c in range(QT):
+            for t in range(PACK - 1):
+                multiply(t, c)
+        for c in range(QT):
+            multiply(PACK - 1, c)
+        o_grouped = tile("o_grouped", [P, QT, P, PACK], BF16)
+        result = tile("result", [P, PACK, Q], F32)
+        nc.vector.tensor_copy(o_grouped[:, 0], out_ps[0][:].rearrange("p t q -> p q t"))
+        nc.scalar.copy(o_grouped[:, 1], out_ps[1][:].rearrange("p t q -> p q t"))
+        nc.vector.tensor_copy(result[:, :, 0:P], out_ps[0][:])
+        nc.scalar.copy(result[:, :, P : 2 * P], out_ps[1][:])
+        nc.sync.dma_start(out_0.rearrange("(p t) q -> p t q", t=PACK), result[:])
 
         o_codes = tile("o_codes", [P, Q], U32)
         o_scales = tile("o_scales", [P, Q], U8)

@@ -104,7 +104,7 @@ def tile_attend_expiringslots_pl_kernel(
         q_codes, q_scales = both_codes[:, Q : 2 * Q], both_scales[:, Q : 2 * Q]
 
         def gather_values(t):
-            picked = tile("picked%d" % t, [P, I], BF16, tag=("q_grouped", "both_scales", None, "p1")[t])
+            picked = tile("picked%d" % t, [P, I], BF16, tag=("q_grouped", None, None, "left0")[t])
             nc.vector.tensor_copy(picked[:], val_pools[t][:].indirect(offsets[:]))
             return picked
 
@@ -120,8 +120,22 @@ def tile_attend_expiringslots_pl_kernel(
 
         picked0 = gather_values(0)
 
+        def scores(c):
+            cols = slice(P * c, P * (c + 1))
+            score_ps = bank("score%d" % c, "score_ps%d" % c, [P, I])
+            nc.tensor.matmul_mx(
+                score_ps[:],
+                lhsT=q_codes[:, cols].bitcast(FP8X4),
+                lhsT_scale=q_scales[:, cols],
+                rhs=key_words[:].bitcast(FP4X4),
+                rhs_scale=key_scales[:],
+                start=True,
+                stop=True,
+            )
+            return score_ps
+
         short = tile("short", [P, 4, Q], F32)
-        score_banks = []
+        score_banks = [scores(0)]
         for h in range(2):
             life_ps = bank("life%d" % h, "life_ps%d" % h, [P, 2, Q])
             for jj in range(2):
@@ -135,36 +149,26 @@ def tile_attend_expiringslots_pl_kernel(
                     start=True,
                     stop=True,
                 )
-            cols = slice(P * h, P * (h + 1))
-            score_ps = bank("score%d" % h, "score_ps%d" % h, [P, I])
-            nc.tensor.matmul_mx(
-                score_ps[:],
-                lhsT=q_codes[:, cols].bitcast(FP8X4),
-                lhsT_scale=q_scales[:, cols],
-                rhs=key_words[:].bitcast(FP4X4),
-                rhs_scale=key_scales[:],
-                start=True,
-                stop=True,
-            )
-            score_banks.append(score_ps)
             for jj in range(2):
                 j = 2 * h + jj
                 nc.scalar.activation(
                     short[:, j, :], life_ps[:, jj, :], ACT.Identity, bias=age_cols[:, j : j + 1], scale=-1.0
                 )
+        score_banks.append(scores(1))
 
         def exponentials(c):
-            neg_max = tile("neg_max%d" % c, [P, 1], F32, tag="pool0" if c == 0 else None)
+            neg_max = tile("neg_max%d" % c, [P, 1], F32, tag="pool%d" % c)
             nc.vector.tensor_reduce(neg_max[:], score_banks[c][:], AXIS.X, ALU.max, negate=True)
             ex = tile("exp%d" % c, [P, I], F32)
             nc.scalar.activation(ex[:], score_banks[c][:], ACT.Exp, bias=neg_max[:], scale=1.0)
             return ex
 
-        exps = [exponentials(c) for c in range(QT)]
+        exps = [exponentials(0)]
+        picked1 = gather_values(1)
+        exps.append(exponentials(1))
 
         val_pools.append(load_values(3))
         turned = [turn_values(0, picked0)]
-        picked1 = gather_values(1)
         picked2 = gather_values(2)
 
         ps_tiles = []
@@ -176,7 +180,7 @@ def tile_attend_expiringslots_pl_kernel(
                 nc.tensor.transpose(back_ps[:, P * j : P * (j + 1)], short[:, j, cols], ident[:])
             left = tile("left%d" % c, [P, I], F32)
             nc.scalar.activation(left[:], back_ps[:], ACT.Relu, bias=grace_cols[:, c : c + 1], scale=-1.0)
-            p = tile("p%d" % c, [P, I], F32, tag="pool2" if c == 0 else None)
+            p = tile("p%d" % c, [P, I], F32, tag=("pool2", "left0")[c])
             nc.vector.scalar_tensor_tensor(
                 p[:], left[:], 1.0, exps[c][:], ALU.min, ALU.mult, accum_out=totals[:, c : c + 1]
             )
@@ -210,7 +214,7 @@ def tile_attend_expiringslots_pl_kernel(
         turned.append(turn_values(3, picked3))
 
         def quantise_values(t):
-            v_codes = tile("v_codes%d" % t, [P, P], U32, tag=("left0", "left1", "pool2", None)[t])
+            v_codes = tile("v_codes%d" % t, [P, P], U32, tag=("exp0", "left1", "pool2", None)[t])
             v_scales = tile("v_scales%d" % t, [P, P], U8)
             nc.vector.quantize_mx(v_codes[:].bitcast(FP8X4), v_scales[:], turned[t][:])
             return v_codes, v_scales
@@ -218,42 +222,34 @@ def tile_attend_expiringslots_pl_kernel(
         v_mx = [quantise_values(t) for t in range(PACK - 1)]
         w_codes = tile("w_codes", [P, Q], U32)
         w_scales = tile("w_scales", [P, Q], U8)
-        for c in range(QT):
-            cols = slice(P * c, P * (c + 1))
-            nc.vector.quantize_mx(w_codes[:, cols].bitcast(FP8X4), w_scales[:, cols], wt[:, c, :])
+        nc.vector.quantize_mx(w_codes[:].bitcast(FP8X4), w_scales[:], wt[:].rearrange("s c x -> s (c x)"))
         v_mx.append(quantise_values(PACK - 1))
 
-        out_ps = [bank("score%d" % c, "out_ps%d" % c, [P, PACK, P]) for c in range(QT)]
-
-        def multiply(t, c):
-            cols = slice(P * c, P * (c + 1))
-            nc.tensor.matmul_mx(
-                out_ps[c][:, t, :],
-                lhsT=v_mx[t][0][:].bitcast(FP8X4),
-                lhsT_scale=v_mx[t][1][:],
-                rhs=w_codes[:, cols].bitcast(FP8X4),
-                rhs_scale=w_scales[:, cols],
-                start=True,
-                stop=True,
-            )
-
-        for c in range(QT):
-            for t in range(PACK - 1):
-                multiply(t, c)
-        for c in range(QT):
-            multiply(PACK - 1, c)
-        o_grouped = tile("o_grouped", [P, QT, P, PACK], BF16)
-        result = tile("result", [P, PACK, Q], F32)
-        nc.vector.tensor_copy(o_grouped[:, 0], out_ps[0][:].rearrange("p t q -> p q t"))
-        nc.scalar.copy(o_grouped[:, 1], out_ps[1][:].rearrange("p t q -> p q t"))
-        nc.vector.tensor_copy(result[:, :, 0:P], out_ps[0][:])
-        nc.scalar.copy(result[:, :, P : 2 * P], out_ps[1][:])
-        nc.sync.dma_start(out_0.rearrange("(p t) q -> p t q", t=PACK), result[:])
+        out_dealt = out_0.rearrange("(p h t) q -> h p t q", h=2, t=2)
+        o_grouped = tile("o_grouped", [P, Q, PACK], BF16)
+        for h in range(2):
+            out_ps = bank("score%d" % h, "out_ps%d" % h, [P, 2, Q])
+            for tt in range(2):
+                v_codes, v_scales = v_mx[2 * h + tt]
+                nc.tensor.matmul_mx(
+                    out_ps[:, tt, :],
+                    lhsT=v_codes[:].bitcast(FP8X4),
+                    lhsT_scale=v_scales[:],
+                    rhs=w_codes[:].bitcast(FP8X4),
+                    rhs_scale=w_scales[:],
+                    start=True,
+                    stop=True,
+                )
+            copy_pair = nc.scalar.copy if h == 0 else nc.vector.tensor_copy
+            copy_pair(o_grouped[:, :, 2 * h : 2 * h + 2], out_ps[:].rearrange("p t q -> p q t"))
+            result = tile("result%d" % h, [P, 2, Q], F32)
+            nc.scalar.copy(result[:], out_ps[:])
+            nc.sync.dma_start(out_dealt[h], result[:])
 
         o_codes = tile("o_codes", [P, Q], U32)
         o_scales = tile("o_scales", [P, Q], U8)
         nc.vector.quantize_mx(
-            o_codes[:].bitcast(FP8X4), o_scales[:], o_grouped[:].rearrange("p c q t -> p (c q t)")
+            o_codes[:].bitcast(FP8X4), o_scales[:], o_grouped[:].rearrange("p q t -> p (q t)")
         )
         nc.sync.dma_start(out_1[0].rearrange("p c r -> p (c r)").bitcast(I32), o_codes[:].bitcast(I32))
         for g in range(4):

from contextlib import ExitStack

import concourse.mybir as mybir
from concourse.masks import make_identity

D, T, I, Q, E = 512, 2048, 512, 256, 512
FLOPS = 2 * D * Q * I * 2 + 2 * I * E * Q
BYTES = 4 * (2 * D * Q + T + Q + I + E * T + E * Q) + 128 * 2 * T + 16 * T + 128 * 64 + 128 * Q * 4 + 16 * Q

F32 = mybir.dt.float32
BF16 = mybir.dt.bfloat16
I32 = mybir.dt.int32
U32 = mybir.dt.uint32
U16 = mybir.dt.uint16
U8 = mybir.dt.uint8
FP8X4 = mybir.dt.float8_e4m3fn_x4
FP4X4 = mybir.dt.float4_e2m1fn_x4
ACT = mybir.ActivationFunctionType
ALU = mybir.AluOpType
AXIS = mybir.AxisListType

P = 128
PACK = 4
QT = Q // P


def tile_attend_expiringslots_pl_kernel(
    tc, query, lquery, keys_words, keys_scales, age, grace, size, vals, offs, out_0, out_1, out_2
):
    nc = tc.nc
    with ExitStack() as ctx:
        sb = ctx.enter_context(tc.tile_pool(name="sb", bufs=1))
        ps = ctx.enter_context(tc.psum_pool(name="ps", bufs=1))

        def tile(name, shape, dtype, tag=None):
            return sb.tile(shape, dtype, name=name, tag=tag or name, align_bytes=64)

        def bank(tag, name, shape):
            return ps.tile(shape, F32, name=name, tag=tag)

        offsets = tile("offsets", [P, I // 16], U16)
        key_scale_pool = tile("key_scale_pool", [P, T], U8, tag="small")
        lq_raw = tile("lq_raw", [P, PACK, Q], F32, tag="pool1")
        age_pool = tile("age_pool", [P, T], F32, tag="pool3")
        key_word_pool = tile("key_word_pool", [P, T], U16, tag="pool0")
        q_raw = tile("q_raw", [P, PACK, Q], F32, tag="pool2")
        age_row = tile("age_row", [P, I], F32)
        ident = tile("ident", [P, P], F32)

        nc.sync.dma_start(offsets[:], offs)
        nc.sync.dma_start(key_word_pool[:].bitcast(I32), keys_words[0].bitcast(I32))
        nc.sync.dma_start(lq_raw[:], lquery.rearrange("(p j) q -> p j q", j=PACK))
        nc.sync.dma_start(q_raw[:], query.rearrange("(p j) q -> p j q", j=PACK))
        nc.gpsimd.memset(key_scale_pool[:].bitcast(I32), 0)
        nc.vector.memset(age_pool[:].bitcast(I32), 0)
        make_identity(nc, ident[:])
        for g in range(4):
            nc.scalar.dma_start(
                key_scale_pool[32 * g : 32 * g + 4, :].bitcast(I32),
                keys_scales[0, 4 * g : 4 * g + 4, :].bitcast(I32),
            )
        nc.scalar.dma_start(age_pool[0:1, :], age[0:1, :])
        vals_dealt = vals.rearrange("(p t) n -> t p n", t=PACK)

        def load_values(t):
            pool = tile("val_pool%d" % t, [P, T], F32, tag="pool%d" % t)
            nc.sync.dma_start(pool[:], vals_dealt[t])
            return pool

        key_scales = tile("key_scales", [P, I], U8)
        key_words = tile("key_words", [P, I], U16)
        nc.vector.tensor_copy(key_words[:], key_word_pool[:].indirect(offsets[:]))
        nc.vector.tensor_copy(key_scales[:], key_scale_pool[:].indirect(offsets[:]))
        nc.vector.tensor_copy(age_row[:], age_pool[:].indirect(offsets[:]))
        val_pools = [load_values(0)]
        small = tile("small", [P, 16], F32, tag="small")
        size_cols = small[:, 0:PACK]
        grace_cols = small[:, 8 : 8 + QT]
        nc.sync.dma_start(size_cols, size.rearrange("o (p c) -> p (o c)", c=PACK))
        with nc.allow_non_contiguous_dma(reason="one grace to a partition"):
            nc.sync.dma_start(grace_cols, grace.rearrange("(c p) o -> p (c o)", p=P))

        age_ps = bank("turn", "age_ps", [P, 4, P])
        for j in range(4):
            nc.tensor.transpose(age_ps[:, j, :], age_row[:, P * j : P * (j + 1)], ident[:])
        age_cols = tile("age_cols", [P, 4], F32)
        nc.scalar.copy(age_cols[:], age_ps[:, :, 0])

        grouped = tile("q_grouped", [P, 2, Q, PACK], BF16)
        for n, raw in enumerate((lq_raw, q_raw)):
            nc.scalar.activation(
                grouped[:, n].rearrange("p (c i) j -> p c j i", i=4),
                raw[:].rearrange("p j (c i) -> p c j i", i=4),
                ACT.Copy,
            )
        val_pools.append(load_values(1))
        val_pools.append(load_values(2))
        both_codes = tile("both_codes", [P, 2 * Q], U32, tag="pool3")
        both_scales = tile("both_scales", [P, 2 * Q], U8)
        nc.vector.quantize_mx(
            both_codes[:].bitcast(FP8X4), both_scales[:], grouped[:].rearrange("p n q j -> p (n q j)")
        )
        lq_codes, lq_scales = both_codes[:, 0:Q], both_scales[:, 0:Q]
        q_codes, q_scales = both_codes[:, Q : 2 * Q], both_scales[:, Q : 2 * Q]

        def gather_values(t):
            picked = tile("picked%d" % t, [P, I], BF16, tag=("q_grouped", None, None, "left0")[t])
            nc.vector.tensor_copy(picked[:], val_pools[t][:].indirect(offsets[:]))
            return picked

        def turn_values(t, picked):
            vt_ps = bank("turn", "vt_ps%d" % t, [P, 2, P])
            for u in range(2):
                nc.tensor.transpose(vt_ps[:, u, :], picked[:].bitcast(F32)[:, u::2], ident[:])
            vt = tile("vt%d" % t, [P, P * PACK], BF16)
            nc.scalar.copy(
                vt[:].bitcast(F32).rearrange("s (e u) -> s e u", u=2), vt_ps[:].rearrange("s u e -> s e u")
            )
            return vt

        picked0 = gather_values(0)

        def scores(c):
            cols = slice(P * c, P * (c + 1))
            score_ps = bank("score%d" % c, "score_ps%d" % c, [P, I])
            nc.tensor.matmul_mx(
                score_ps[:],
                lhsT=q_codes[:, cols].bitcast(FP8X4),
                lhsT_scale=q_scales[:, cols],
                rhs=key_words[:].bitcast(FP4X4),
                rhs_scale=key_scales[:],
                start=True,
                stop=True,
            )
            return score_ps

        short = tile("short", [P, 4, Q], F32)
        score_banks = [scores(0)]
        for h in range(2):
            life_ps = bank("life%d" % h, "life_ps%d" % h, [P, 2, Q])
            for jj in range(2):
                cols = slice(P * (2 * h + jj), P * (2 * h + jj + 1))
                nc.tensor.matmul_mx(
                    life_ps[:, jj, :],
                    lhsT=key_words[:, cols].bitcast(FP4X4),
                    lhsT_scale=key_scales[:, cols],
                    rhs=lq_codes.bitcast(FP8X4),
                    rhs_scale=lq_scales,
                    start=True,
                    stop=True,
                )
            for jj in range(2):
                j = 2 * h + jj
                nc.scalar.activation(
                    short[:, j, :], life_ps[:, jj, :], ACT.Identity, bias=age_cols[:, j : j + 1], scale=-1.0
                )
        score_banks.append(scores(1))

        def exponentials(c):
            neg_max = tile("neg_max%d" % c, [P, 1], F32, tag="pool%d" % c)
            nc.vector.tensor_reduce(neg_max[:], score_banks[c][:], AXIS.X, ALU.max, negate=True)
            ex = tile("exp%d" % c, [P, I], F32)
            nc.scalar.activation(ex[:], score_banks[c][:], ACT.Exp, bias=neg_max[:], scale=1.0)
            return ex

        exps = [exponentials(0)]
        picked1 = gather_values(1)
        exps.append(exponentials(1))

        val_pools.append(load_values(3))
        turned = [turn_values(0, picked0)]
        picked2 = gather_values(2)

        ps_tiles = []
        totals = tile("totals", [P, QT], F32)
        for c in range(QT):
            cols = slice(P * c, P * (c + 1))
            back_ps = bank("back%d" % c, "back_ps%d" % c, [P, I])
            for j in range(4):
                nc.tensor.transpose(back_ps[:, P * j : P * (j + 1)], short[:, j, cols], ident[:])
            left = tile("left%d" % c, [P, I], F32)
            nc.scalar.activation(left[:], back_ps[:], ACT.Relu, bias=grace_cols[:, c : c + 1], scale=-1.0)
            p = tile("p%d" % c, [P, I], F32, tag=("pool2", "left0")[c])
            nc.vector.scalar_tensor_tensor(
                p[:], left[:], 1.0, exps[c][:], ALU.min, ALU.mult, accum_out=totals[:, c : c + 1]
            )
            ps_tiles.append(p)
        turned.append(turn_values(1, picked1))
        turned.append(turn_values(2, picked2))
        size_ps = bank("life0", "size_ps", [P, PACK, P])
        for c in range(PACK):
            nc.tensor.transpose(size_ps[:, c, :], size_cols[:, c : c + 1].to_broadcast([P, P]), ident[:])

        inv = tile("inv", [P, QT], F32)
        nc.vector.reciprocal(inv[:], totals[:])
        wt = tile("wt", [P, QT, P * PACK], BF16)
        for c in range(QT):
            w = tile("w%d" % c, [P, I], BF16)
            nc.vector.scalar_tensor_tensor(
                w[:].rearrange("q (s r) -> q s r", r=PACK),
                ps_tiles[c][:].rearrange("q (s r) -> q s r", r=PACK),
                inv[:, c : c + 1],
                size_ps[:].rearrange("q r s -> q s r"),
                ALU.mult,
                ALU.mult,
            )
            wt_ps = bank(("spare", "life1")[c], "wt_ps%d" % c, [P, 2, P])
            for u in range(2):
                nc.tensor.transpose(wt_ps[:, u, :], w[:].bitcast(F32)[:, u::2], ident[:])
            nc.scalar.copy(
                wt[:, c, :].bitcast(F32).rearrange("s (q u) -> s q u", u=2), wt_ps[:].rearrange("s u q -> s q u")
            )
        picked3 = gather_values(3)
        turned.append(turn_values(3, picked3))

        def quantise_values(t):
            v_codes = tile("v_codes%d" % t, [P, P], U32, tag=("exp0", "left1", "pool2", None)[t])
            v_scales = tile("v_scales%d" % t, [P, P], U8)
            nc.vector.quantize_mx(v_codes[:].bitcast(FP8X4), v_scales[:], turned[t][:])
            return v_codes, v_scales

        v_mx = [quantise_values(t) for t in range(PACK - 1)]
        w_codes = tile("w_codes", [P, Q], U32)
        w_scales = tile("w_scales", [P, Q], U8)
        nc.vector.quantize_mx(w_codes[:].bitcast(FP8X4), w_scales[:], wt[:].rearrange("s c x -> s (c x)"))
        v_mx.append(quantise_values(PACK - 1))

        out_dealt = out_0.rearrange("(p h t) q -> h p t q", h=2, t=2)
        o_grouped = tile("o_grouped", [P, Q, PACK], BF16)
        for h in range(2):
            out_ps = bank("score%d" % h, "out_ps%d" % h, [P, 2, Q])
            for tt in range(2):
                v_codes, v_scales = v_mx[2 * h + tt]
                nc.tensor.matmul_mx(
                    out_ps[:, tt, :],
                    lhsT=v_codes[:].bitcast(FP8X4),
                    lhsT_scale=v_scales[:],
                    rhs=w_codes[:].bitcast(FP8X4),
                    rhs_scale=w_scales[:],
                    start=True,
                    stop=True,
                )
            copy_pair = nc.scalar.copy if h == 0 else nc.vector.tensor_copy
            copy_pair(o_grouped[:, :, 2 * h : 2 * h + 2], out_ps[:].rearrange("p t q -> p q t"))
            result = tile("result%d" % h, [P, 2, Q], F32)
            nc.scalar.copy(result[:], out_ps[:])
            nc.sync.dma_start(out_dealt[h], result[:])

        o_codes = tile("o_codes", [P, Q], U32)
        o_scales = tile("o_scales", [P, Q], U8)
        nc.vector.quantize_mx(
            o_codes[:].bitcast(FP8X4), o_scales[:], o_grouped[:].rearrange("p q t -> p (q t)")
        )
        nc.sync.dma_start(out_1[0].rearrange("p c r -> p (c r)").bitcast(I32), o_codes[:].bitcast(I32))
        for g in range(4):
            queue = nc.sync if g % 2 == 0 else nc.scalar
            queue.dma_start(
                out_2[0, 4 * g : 4 * g + 4, :].bitcast(I32), o_scales[32 * g : 32 * g + 4, :].bitcast(I32)
            )
